import numpy as np, ml_dtypes
CORES = [0,1,2,3,4,5,6,7,8,9,10,11,12,13,14,15]
N = 16
ROOT = 15
def setup_inputs(rng):
    return {"x": rng.standard_normal((N, 128, 512), dtype=np.float32).astype(ml_dtypes.bfloat16)}
def reference(x):
    y = np.full((N, 128, N * 512), np.nan, x.dtype)
    y[ROOT] = np.concatenate(list(x), axis=1)
    return {"y": y}

@@ -1,0 +1,62 @@
+from concourse.bass import DstId, RemoteDMATransfer
+B = 512
+H = B // 2
+ROOT = 15
+HAND = {0: (2, 6, 0), 1: (3, 7, 0), 4: (2, 6, 1), 5: (2, 6, 2)}
+SCRATCH = {'xs': ('sbuf', [128, B], 'bfloat16'), 'rel0': ('sbuf', [128, H], 'bfloat16'), 'rel1': ('sbuf', [128, H], 'bfloat16'), 'rel2': ('sbuf', [128, H], 'bfloat16'), 'land': ('sbuf', [128, 16 * B], 'bfloat16')}
+SEMAPHORES = ['loaded', 'loaded2', 'sent', 'handed0', 'handed1', 'handed2', 'near', 'g67', 'g0123', 'g4', 'g5', 'stored']
+
+def rank_program(g, core, T, topo):
+    s = T.sem
+    rel = (T.rel0, T.rel1, T.rel2)
+    handed = (s.handed0, s.handed1, s.handed2)
+
+    def cols(t, a, b):
+        return t[:, a * B:b * B]
+
+    def send(dst, out_ap, in_ap, remote_sem):
+        rid, pid, _se = topo.addr(dst)
+        g.remote_dma(out_ap, in_ap, remote_sem, s.sent, pid, rid, topo.mask(core, dst))
+    if core == ROOT:
+        g.dma_start(cols(T.y, ROOT, ROOT + 1), T.x[:]).then_inc(s.stored, 16)
+        n = 16
+        for sem, count, a, b in ((s.near, 7 * 16, 8, 15), (s.g67, 4 * 8, 6, 8), (s.g0123, 8 * 8, 0, 4), (s.g4, 2 * 8, 4, 5), (s.g5, 2 * 8, 5, 6)):
+            g.wait_ge(sem, count)
+            g.dma_start(cols(T.y, a, b), cols(T.land, a, b)).then_inc(s.stored, 16)
+            n += 16
+        g.wait_ge(s.stored, n)
+        return
+    if topo.chip(core) == topo.chip(ROOT):
+        g.dma_start(T.xs[:], T.x[:]).then_inc(s.loaded, 16)
+        g.wait_ge(s.loaded, 16)
+        send(ROOT, cols(T.land, core, core + 1), T.xs[:], s.near)
+        g.wait_ge(s.sent, 16)
+    elif core in HAND:
+        g.dma_start(T.xs[:], T.x[:]).then_inc(s.loaded, 16)
+        g.wait_ge(s.loaded, 16)
+        slot = HAND[core][2]
+        trs = []
+        for k in (0, 1):
+            rid, pid, _se = topo.addr(HAND[core][k])
+            trs.append(RemoteDMATransfer(dst_ids=[DstId(rid=rid, pnc=pid)], dma_engine_mask=255 << 8 * k, remote_sem=handed[slot], src=T.xs[:, k * H:(k + 1) * H], dst=rel[slot][:]))
+        g.remote_dma_fused(trs, local_sem=s.sent)
+        g.wait_ge(s.sent, 16)
+    else:
+        own = s.g67 if core >= 6 else s.g0123
+        for k, sem in ((0, s.loaded), (1, s.loaded2)):
+            g.dma_start(T.xs[:, k * H:(k + 1) * H], T.x[:, k * H:(k + 1) * H]).then_inc(sem, 16)
+        n = 0
+        for k, sem in ((0, s.loaded), (1, s.loaded2)):
+            g.wait_ge(sem, 16)
+            c0 = core * B + k * H
+            send(ROOT, T.land[:, c0:c0 + H], T.xs[:, k * H:(k + 1) * H], own)
+            n += 8
+        group = {0: s.g0123, 1: s.g0123, 4: s.g4, 5: s.g5}
+        for slot in (0, 1, 2):
+            for h in sorted(HAND):
+                if HAND[h][2] == slot and core in HAND[h][:2]:
+                    c0 = h * B + HAND[h][:2].index(core) * H
+                    g.wait_ge(handed[slot], 8)
+                    send(ROOT, T.land[:, c0:c0 + H], rel[slot][:], group[h])
+                    n += 8
+        g.wait_ge(s.sent, n)

@@ -18,21 +18,23 @@ def rank_program(g, core, T, topo):
         rid, pid, _se = topo.addr(dst)
         g.remote_dma(out_ap, in_ap, remote_sem, s.sent, pid, rid, topo.mask(core, dst))
     if core == ROOT:
-        g.dma_start(cols(T.y, ROOT, ROOT + 1), T.x[:]).then_inc(s.stored, 16)
+        g.scalar.dma_start(cols(T.y, ROOT, ROOT + 1), T.x[:]).then_inc(s.stored, 16)
         n = 16
-        for sem, count, a, b in ((s.near, 7 * 16, 8, 15), (s.g67, 4 * 8, 6, 8), (s.g0123, 8 * 8, 0, 4), (s.g4, 2 * 8, 4, 5), (s.g5, 2 * 8, 5, 6)):
-            g.wait_ge(sem, count)
-            g.dma_start(cols(T.y, a, b), cols(T.land, a, b)).then_inc(s.stored, 16)
+        qs = (g.sync, g.scalar)
+        for i, (sem, count, a, b) in enumerate(((s.near, 7 * 16, 8, 15), (s.g67, 4 * 8, 6, 8), (s.g0123, 8 * 8, 0, 4), (s.g4, 2 * 8, 4, 5), (s.g5, 2 * 8, 5, 6))):
+            q = qs[i % 2]
+            q.wait_ge(sem, count)
+            q.dma_start(cols(T.y, a, b), cols(T.land, a, b)).then_inc(s.stored, 16)
             n += 16
         g.wait_ge(s.stored, n)
         return
     if topo.chip(core) == topo.chip(ROOT):
-        g.dma_start(T.xs[:], T.x[:]).then_inc(s.loaded, 16)
+        g.sync.dma_start(T.xs[:], T.x[:]).then_inc(s.loaded, 16)
         g.wait_ge(s.loaded, 16)
         send(ROOT, cols(T.land, core, core + 1), T.xs[:], s.near)
         g.wait_ge(s.sent, 16)
     elif core in HAND:
-        g.dma_start(T.xs[:], T.x[:]).then_inc(s.loaded, 16)
+        g.sync.dma_start(T.xs[:], T.x[:]).then_inc(s.loaded, 16)
         g.wait_ge(s.loaded, 16)
         slot = HAND[core][2]
         trs = []
@@ -43,8 +45,8 @@ def rank_program(g, core, T, topo):
         g.wait_ge(s.sent, 16)
     else:
         own = s.g67 if core >= 6 else s.g0123
-        for k, sem in ((0, s.loaded), (1, s.loaded2)):
-            g.dma_start(T.xs[:, k * H:(k + 1) * H], T.x[:, k * H:(k + 1) * H]).then_inc(sem, 16)
+        for k, sem, q in ((0, s.loaded, g.sync), (1, s.loaded2, g.scalar)):
+            q.dma_start(T.xs[:, k * H:(k + 1) * H], T.x[:, k * H:(k + 1) * H]).then_inc(sem, 16)
         n = 0
         for k, sem in ((0, s.loaded), (1, s.loaded2)):
             g.wait_ge(sem, 16)

@@ -1,64 +1,94 @@
 from concourse.bass import DstId, RemoteDMATransfer
 B = 512
-H = B // 2
 ROOT = 15
-HAND = {0: (2, 6, 0), 1: (3, 7, 0), 4: (2, 6, 1), 5: (2, 6, 2)}
-SCRATCH = {'xs': ('sbuf', [128, B], 'bfloat16'), 'rel0': ('sbuf', [128, H], 'bfloat16'), 'rel1': ('sbuf', [128, H], 'bfloat16'), 'rel2': ('sbuf', [128, H], 'bfloat16'), 'land': ('sbuf', [128, 16 * B], 'bfloat16')}
-SEMAPHORES = ['loaded', 'loaded2', 'sent', 'handed0', 'handed1', 'handed2', 'near', 'g67', 'g0123', 'g4', 'g5', 'stored']
+PLAN = {
+    2: [(2, 0, 256), (2, 256, 512), (0, 0, 256), (4, 0, 256), (5, 0, 256)],
+    6: [(6, 0, 256), (6, 256, 512), (0, 256, 512), (4, 256, 512), (5, 256, 512)],
+    3: [(3, 0, 256), (3, 256, 512), (1, 0, 256)],
+    7: [(7, 0, 256), (7, 256, 512), (1, 256, 512)],
+    14: [(14, 0, 512), (12, 0, 512), (10, 0, 512), (8, 0, 256)],
+    13: [(13, 0, 512), (11, 0, 512), (9, 0, 512), (8, 256, 512)],
+}
+STORES = [(13 * B, 15 * B, 0), (11 * B, 13 * B, 0), (9 * B, 11 * B, 0), (8 * B, 9 * B, 0),
+          (6 * B, 8 * B, 1), (0, 4 * B, 1), (4 * B, 5 * B, 1), (5 * B, 6 * B, 1)]
+SCRATCH = {'xs': ('sbuf', [128, B], 'bfloat16'), 'rel': ('sbuf', [128, 4 * B], 'bfloat16'),
+           'land': ('sbuf', [128, 16 * B], 'bfloat16')}
+SEMAPHORES = (['sent', 'stored', 'own'] + ['ld%d' % i for i in range(8)] + ['h%d' % i for i in range(8)]
+              + ['st%d' % i for i in range(12)])
+
+
+def store_of(a, b):
+    for i, (lo, hi, _q) in enumerate(STORES):
+        if lo <= a and b <= hi:
+            return i
+    raise ValueError((a, b))
+
 
 def rank_program(g, core, T, topo):
     s = T.sem
-    rel = (T.rel0, T.rel1, T.rel2)
-    handed = (s.handed0, s.handed1, s.handed2)
+    LD = (s.ld0, s.ld1, s.ld2, s.ld3, s.ld4, s.ld5, s.ld6, s.ld7)
+    HS = (s.h0, s.h1, s.h2, s.h3, s.h4, s.h5, s.h6, s.h7)
+    ST = (s.st0, s.st1, s.st2, s.st3, s.st4, s.st5, s.st6, s.st7, s.st8, s.st9, s.st10, s.st11)
+    qs = (g.sync, g.scalar)
 
-    def cols(t, a, b):
-        return t[:, a * B:b * B]
+    def width(src):
+        return 16 if topo.chip(src) == topo.chip(ROOT) else 8
 
     def send(dst, out_ap, in_ap, remote_sem):
         rid, pid, _se = topo.addr(dst)
         g.remote_dma(out_ap, in_ap, remote_sem, s.sent, pid, rid, topo.mask(core, dst))
+
     if core == ROOT:
-        g.scalar.dma_start(cols(T.y, ROOT, ROOT + 1), T.x[:]).then_inc(s.stored, 16)
-        n = 16
-        qs = (g.sync, g.scalar)
-        for i, (sem, count, a, b) in enumerate(((s.near, 7 * 16, 8, 15), (s.g67, 4 * 8, 6, 8), (s.g0123, 8 * 8, 0, 4), (s.g4, 2 * 8, 4, 5), (s.g5, 2 * 8, 5, 6))):
-            q = qs[i % 2]
-            q.wait_ge(sem, count)
-            q.dma_start(cols(T.y, a, b), cols(T.land, a, b)).then_inc(s.stored, 16)
-            n += 16
-        g.wait_ge(s.stored, n)
+        need = [0] * len(STORES)
+        for src, plan in PLAN.items():
+            for blk, a, b in plan:
+                need[store_of(blk * B + a, blk * B + b)] += width(src)
+        g.dma_start(T.y[:, ROOT * B:(ROOT + 1) * B], T.x[:]).then_inc(s.own, 16)
+        for i, (lo, hi, q) in enumerate(STORES):
+            qs[q].wait_ge(ST[i], need[i])
+            qs[q].dma_start(T.y[:, lo:hi], T.land[:, lo:hi]).then_inc(s.stored, 16)
+        g.wait_ge(s.own, 16)
+        g.wait_ge(s.stored, 16 * len(STORES))
         return
-    if topo.chip(core) == topo.chip(ROOT):
-        g.sync.dma_start(T.xs[:], T.x[:]).then_inc(s.loaded, 16)
-        g.wait_ge(s.loaded, 16)
-        send(ROOT, cols(T.land, core, core + 1), T.xs[:], s.near)
-        g.wait_ge(s.sent, 16)
-    elif core in HAND:
-        g.sync.dma_start(T.xs[:], T.x[:]).then_inc(s.loaded, 16)
-        g.wait_ge(s.loaded, 16)
-        slot = HAND[core][2]
+    if core not in PLAN:
+        g.sync.dma_start(T.xs[:], T.x[:]).then_inc(s.ld0, 16)
+        g.wait_ge(s.ld0, 16)
+        pieces = []
+        for gate, plan in PLAN.items():
+            off = 0
+            for i, (blk, a, b) in enumerate(plan):
+                if blk == core:
+                    pieces.append((i, gate, a, b, off))
+                if blk != gate:
+                    off += b - a
+        pieces.sort()
+        ne = 16 // len(pieces)
         trs = []
-        for k in (0, 1):
-            rid, pid, _se = topo.addr(HAND[core][k])
-            trs.append(RemoteDMATransfer(dst_ids=[DstId(rid=rid, pnc=pid)], dma_engine_mask=255 << 8 * k, remote_sem=handed[slot], src=T.xs[:, k * H:(k + 1) * H], dst=rel[slot][:]))
+        for k, (i, gate, a, b, off) in enumerate(pieces):
+            rid, pid, _se = topo.addr(gate)
+            trs.append(RemoteDMATransfer(dst_ids=[DstId(rid=rid, pnc=pid)],
+                                         dma_engine_mask=((1 << ne) - 1) << (ne * k),
+                                         remote_sem=HS[i], src=T.xs[:, a:b],
+                                         dst=T.rel[:, off:off + b - a]))
         g.remote_dma_fused(trs, local_sem=s.sent)
         g.wait_ge(s.sent, 16)
-    else:
-        own = s.g67 if core >= 6 else s.g0123
-        for k, sem, q in ((0, s.loaded, g.sync), (1, s.loaded2, g.scalar)):
-            q.dma_start(T.xs[:, k * H:(k + 1) * H], T.x[:, k * H:(k + 1) * H]).then_inc(sem, 16)
-        n = 0
-        for k, sem in ((0, s.loaded), (1, s.loaded2)):
-            g.wait_ge(sem, 16)
-            c0 = core * B + k * H
-            send(ROOT, T.land[:, c0:c0 + H], T.xs[:, k * H:(k + 1) * H], own)
-            n += 8
-        group = {0: s.g0123, 1: s.g0123, 4: s.g4, 5: s.g5}
-        for slot in (0, 1, 2):
-            for h in sorted(HAND):
-                if HAND[h][2] == slot and core in HAND[h][:2]:
-                    c0 = h * B + HAND[h][:2].index(core) * H
-                    g.wait_ge(handed[slot], 8)
-                    send(ROOT, T.land[:, c0:c0 + H], rel[slot][:], group[h])
-                    n += 8
-        g.wait_ge(s.sent, n)
+        return
+    plan = PLAN[core]
+    k = 0
+    for i, (blk, a, b) in enumerate(plan):
+        if blk == core:
+            qs[k % 2].dma_start(T.xs[:, a:b], T.x[:, a:b]).then_inc(LD[i], 16)
+            k += 1
+    off = 0
+    for i, (blk, a, b) in enumerate(plan):
+        dst = T.land[:, blk * B + a:blk * B + b]
+        rs = ST[store_of(blk * B + a, blk * B + b)]
+        if blk == core:
+            g.wait_ge(LD[i], 16)
+            send(ROOT, dst, T.xs[:, a:b], rs)
+        else:
+            nh = sum(1 for p in PLAN.values() for q in p if q[0] == blk)
+            g.wait_ge(HS[i], 16 // nh)
+            send(ROOT, dst, T.rel[:, off:off + b - a], rs)
+            off += b - a
+    g.wait_ge(s.sent, width(core) * len(plan))

@@ -1,6 +1,10 @@
 from concourse.bass import DstId, RemoteDMATransfer
 B = 512
 ROOT = 15
+NS = 8
+RS = 128 // NS
+D = -1
+SLOW = ()
 PLAN = {
     2: [(2, 0, 256), (2, 256, 512), (0, 0, 256), (4, 0, 256), (5, 0, 256)],
     6: [(6, 0, 256), (6, 256, 512), (0, 256, 512), (4, 256, 512), (5, 256, 512)],
@@ -10,18 +14,31 @@ PLAN = {
     13: [(13, 0, 512), (11, 0, 512), (9, 0, 512), (8, 256, 512)],
 }
 STORES = [(13 * B, 15 * B, 0), (11 * B, 13 * B, 0), (9 * B, 11 * B, 0), (8 * B, 9 * B, 0),
-          (6 * B, 8 * B, 1), (0, 4 * B, 1), (4 * B, 5 * B, 1), (5 * B, 6 * B, 1)]
+          (6 * B, 8 * B, 1), (2 * B, 4 * B, 1), (0, 2 * B, 1), (4 * B, 5 * B, 1), (5 * B, 6 * B, 1)]
 SCRATCH = {'xs': ('sbuf', [128, B], 'bfloat16'), 'rel': ('sbuf', [128, 4 * B], 'bfloat16'),
-           'land': ('sbuf', [128, 16 * B], 'bfloat16')}
+           'land': ('sbuf', [128, 16 * B], 'bfloat16'),
+           'xd': ('dram', [NS, 128, B // NS], 'bfloat16'),
+           'dd': ('dram', [8 * NS, 128, B // NS], 'bfloat16')}
 SEMAPHORES = (['sent', 'stored', 'own'] + ['ld%d' % i for i in range(8)] + ['h%d' % i for i in range(8)]
               + ['st%d' % i for i in range(12)])
 
 
-def store_of(a, b):
-    for i, (lo, hi, _q) in enumerate(STORES):
-        if lo <= a and b <= hi:
+def store_of(p):
+    for i, st in enumerate(STORES):
+        if p[1] == D:
+            if st[0] == D and st[1] == p[0] and st[2] <= p[2] and p[3] <= st[3]:
+                return i
+        elif st[0] != D and st[0] <= p[0] * B + p[1] and p[0] * B + p[2] <= st[1]:
             return i
-    raise ValueError((a, b))
+    raise ValueError(p)
+
+
+def parts(p):
+    return p[3] - p[2] if p[1] == D else 1
+
+
+def hand_engines(blk):
+    return 16 // sum(parts(p) for plan in PLAN.values() for p in plan if p[0] == blk)
 
 
 def rank_program(g, core, T, topo):
@@ -30,65 +47,80 @@ def rank_program(g, core, T, topo):
     HS = (s.h0, s.h1, s.h2, s.h3, s.h4, s.h5, s.h6, s.h7)
     ST = (s.st0, s.st1, s.st2, s.st3, s.st4, s.st5, s.st6, s.st7, s.st8, s.st9, s.st10, s.st11)
     qs = (g.sync, g.scalar)
+    lq = (g, g) if core in SLOW else qs
 
     def width(src):
         return 16 if topo.chip(src) == topo.chip(ROOT) else 8
 
-    def send(dst, out_ap, in_ap, remote_sem):
-        rid, pid, _se = topo.addr(dst)
-        g.remote_dma(out_ap, in_ap, remote_sem, s.sent, pid, rid, topo.mask(core, dst))
+    def fused(triples, total):
+        ne = total // len(triples)
+        trs = []
+        for k, (dc, out_ap, in_ap, rs) in enumerate(triples):
+            rid, pid, _se = topo.addr(dc)
+            trs.append(RemoteDMATransfer(dst_ids=[DstId(rid=rid, pnc=pid)],
+                                         dma_engine_mask=((1 << ne) - 1) << (ne * k),
+                                         remote_sem=rs, src=in_ap, dst=out_ap))
+        g.remote_dma_fused(trs, local_sem=s.sent)
 
     if core == ROOT:
         need = [0] * len(STORES)
         for src, plan in PLAN.items():
-            for blk, a, b in plan:
-                need[store_of(blk * B + a, blk * B + b)] += width(src)
+            for p in plan:
+                need[store_of(p)] += width(src)
         g.dma_start(T.y[:, ROOT * B:(ROOT + 1) * B], T.x[:]).then_inc(s.own, 16)
-        for i, (lo, hi, q) in enumerate(STORES):
-            qs[q].wait_ge(ST[i], need[i])
-            qs[q].dma_start(T.y[:, lo:hi], T.land[:, lo:hi]).then_inc(s.stored, 16)
+        for i, st in enumerate(STORES):
+            q = qs[st[-1]]
+            q.wait_ge(ST[i], need[i])
+            if st[0] == D:
+                _d, blk, s0, s1, _q = st
+                q.dma_start(T.y[s0 * RS:s1 * RS, blk * B:(blk + 1) * B],
+                            T.dd[blk * NS + s0:blk * NS + s1]).then_inc(s.stored, 16)
+            else:
+                q.dma_start(T.y[:, st[0]:st[1]], T.land[:, st[0]:st[1]]).then_inc(s.stored, 16)
         g.wait_ge(s.own, 16)
         g.wait_ge(s.stored, 16 * len(STORES))
         return
     if core not in PLAN:
-        g.sync.dma_start(T.xs[:], T.x[:]).then_inc(s.ld0, 16)
-        g.wait_ge(s.ld0, 16)
-        pieces = []
+        trs = []
         for gate, plan in PLAN.items():
             off = 0
-            for i, (blk, a, b) in enumerate(plan):
-                if blk == core:
-                    pieces.append((i, gate, a, b, off))
-                if blk != gate:
-                    off += b - a
-        pieces.sort()
-        ne = 16 // len(pieces)
-        trs = []
-        for k, (i, gate, a, b, off) in enumerate(pieces):
-            rid, pid, _se = topo.addr(gate)
-            trs.append(RemoteDMATransfer(dst_ids=[DstId(rid=rid, pnc=pid)],
-                                         dma_engine_mask=((1 << ne) - 1) << (ne * k),
-                                         remote_sem=HS[i], src=T.xs[:, a:b],
-                                         dst=T.rel[:, off:off + b - a]))
-        g.remote_dma_fused(trs, local_sem=s.sent)
+            for i, p in enumerate(plan):
+                if p[0] == core:
+                    if p[1] == D:
+                        for t in range(p[2], p[3]):
+                            trs.append((i, gate, T.dd[core * NS + t], T.xd[t]))
+                    else:
+                        trs.append((i, gate, T.rel[:, off:off + p[2] - p[1]], T.xs[:, p[1]:p[2]]))
+                if p[0] != gate and p[1] != D:
+                    off += p[2] - p[1]
+        dram = any(p[0] == core and p[1] == D for plan in PLAN.values() for p in plan)
+        lq[0].dma_start(T.xd[:] if dram else T.xs[:], T.x[:]).then_inc(s.ld0, 16)
+        g.wait_ge(s.ld0, 16)
+        fused([(gate, o, i_, HS[i]) for i, gate, o, i_ in trs], 16)
         g.wait_ge(s.sent, 16)
         return
     plan = PLAN[core]
     k = 0
-    for i, (blk, a, b) in enumerate(plan):
-        if blk == core:
-            qs[k % 2].dma_start(T.xs[:, a:b], T.x[:, a:b]).then_inc(LD[i], 16)
+    for i, p in enumerate(plan):
+        if p[0] == core:
+            lq[k % 2].dma_start(T.xs[:, p[1]:p[2]], T.x[:, p[1]:p[2]]).then_inc(LD[i], 16)
             k += 1
     off = 0
-    for i, (blk, a, b) in enumerate(plan):
-        dst = T.land[:, blk * B + a:blk * B + b]
-        rs = ST[store_of(blk * B + a, blk * B + b)]
+    for i, p in enumerate(plan):
+        blk = p[0]
+        rs = ST[store_of(p)]
         if blk == core:
             g.wait_ge(LD[i], 16)
-            send(ROOT, dst, T.xs[:, a:b], rs)
         else:
-            nh = sum(1 for p in PLAN.values() for q in p if q[0] == blk)
-            g.wait_ge(HS[i], 16 // nh)
-            send(ROOT, dst, T.rel[:, off:off + b - a], rs)
-            off += b - a
+            g.wait_ge(HS[i], hand_engines(blk) * parts(p))
+        if p[1] == D:
+            tr = [(ROOT, T.dd[blk * NS + t], T.dd[blk * NS + t], rs) for t in range(p[2], p[3])]
+        else:
+            dst = T.land[:, blk * B + p[1]:blk * B + p[2]]
+            if blk == core:
+                tr = [(ROOT, dst, T.xs[:, p[1]:p[2]], rs)]
+            else:
+                tr = [(ROOT, dst, T.rel[:, off:off + p[2] - p[1]], rs)]
+                off += p[2] - p[1]
+        fused(tr, width(core))
     g.wait_ge(s.sent, width(core) * len(plan))

@@ -1,53 +1,42 @@
 from concourse.bass import DstId, RemoteDMATransfer
 B = 512
+H = 256
 ROOT = 15
-NS = 8
-RS = 128 // NS
-D = -1
-SLOW = ()
 PLAN = {
     2: [(2, 0, 256), (2, 256, 512), (0, 0, 256), (4, 0, 256), (5, 0, 256)],
     6: [(6, 0, 256), (6, 256, 512), (0, 256, 512), (4, 256, 512), (5, 256, 512)],
     3: [(3, 0, 256), (3, 256, 512), (1, 0, 256)],
     7: [(7, 0, 256), (7, 256, 512), (1, 256, 512)],
-    14: [(14, 0, 512), (12, 0, 512), (10, 0, 512), (8, 0, 256)],
-    13: [(13, 0, 512), (11, 0, 512), (9, 0, 512), (8, 256, 512)],
+    14: [(14, 0, 256), (14, 256, 512), (12, 0, 512), (10, 0, 512), (8, 0, 256)],
+    13: [(13, 256, 512), (13, 0, 256), (11, 0, 512), (9, 0, 512), (8, 256, 512)],
 }
-STORES = [(13 * B, 15 * B, 0), (11 * B, 13 * B, 0), (9 * B, 11 * B, 0), (8 * B, 9 * B, 0),
+STORES = [(13 * B + H, 14 * B + H, 0), (14 * B + H, 15 * B, 0), (13 * B, 13 * B + H, 0),
+          (11 * B, 13 * B, 0), (9 * B, 11 * B, 0), (8 * B, 9 * B, 0),
           (6 * B, 8 * B, 1), (2 * B, 4 * B, 1), (0, 2 * B, 1), (4 * B, 5 * B, 1), (5 * B, 6 * B, 1)]
 SCRATCH = {'xs': ('sbuf', [128, B], 'bfloat16'), 'rel': ('sbuf', [128, 4 * B], 'bfloat16'),
-           'land': ('sbuf', [128, 16 * B], 'bfloat16'),
-           'xd': ('dram', [NS, 128, B // NS], 'bfloat16'),
-           'dd': ('dram', [8 * NS, 128, B // NS], 'bfloat16')}
+           'land': ('sbuf', [128, 16 * B], 'bfloat16')}
 SEMAPHORES = (['sent', 'stored', 'own'] + ['ld%d' % i for i in range(8)] + ['h%d' % i for i in range(8)]
-              + ['st%d' % i for i in range(12)])
+              + ['st%d' % i for i in range(16)])
 
 
 def store_of(p):
     for i, st in enumerate(STORES):
-        if p[1] == D:
-            if st[0] == D and st[1] == p[0] and st[2] <= p[2] and p[3] <= st[3]:
-                return i
-        elif st[0] != D and st[0] <= p[0] * B + p[1] and p[0] * B + p[2] <= st[1]:
+        if st[0] <= p[0] * B + p[1] and p[0] * B + p[2] <= st[1]:
             return i
     raise ValueError(p)
 
 
-def parts(p):
-    return p[3] - p[2] if p[1] == D else 1
-
-
 def hand_engines(blk):
-    return 16 // sum(parts(p) for plan in PLAN.values() for p in plan if p[0] == blk)
+    return 16 // sum(1 for plan in PLAN.values() for p in plan if p[0] == blk)
 
 
 def rank_program(g, core, T, topo):
     s = T.sem
     LD = (s.ld0, s.ld1, s.ld2, s.ld3, s.ld4, s.ld5, s.ld6, s.ld7)
     HS = (s.h0, s.h1, s.h2, s.h3, s.h4, s.h5, s.h6, s.h7)
-    ST = (s.st0, s.st1, s.st2, s.st3, s.st4, s.st5, s.st6, s.st7, s.st8, s.st9, s.st10, s.st11)
+    ST = (s.st0, s.st1, s.st2, s.st3, s.st4, s.st5, s.st6, s.st7, s.st8, s.st9, s.st10, s.st11,
+          s.st12, s.st13, s.st14, s.st15)
     qs = (g.sync, g.scalar)
-    lq = (g, g) if core in SLOW else qs
 
     def width(src):
         return 16 if topo.chip(src) == topo.chip(ROOT) else 8
@@ -71,12 +60,7 @@ def rank_program(g, core, T, topo):
         for i, st in enumerate(STORES):
             q = qs[st[-1]]
             q.wait_ge(ST[i], need[i])
-            if st[0] == D:
-                _d, blk, s0, s1, _q = st
-                q.dma_start(T.y[s0 * RS:s1 * RS, blk * B:(blk + 1) * B],
-                            T.dd[blk * NS + s0:blk * NS + s1]).then_inc(s.stored, 16)
-            else:
-                q.dma_start(T.y[:, st[0]:st[1]], T.land[:, st[0]:st[1]]).then_inc(s.stored, 16)
+            q.dma_start(T.y[:, st[0]:st[1]], T.land[:, st[0]:st[1]]).then_inc(s.stored, 16)
         g.wait_ge(s.own, 16)
         g.wait_ge(s.stored, 16 * len(STORES))
         return
@@ -86,41 +70,30 @@ def rank_program(g, core, T, topo):
             off = 0
             for i, p in enumerate(plan):
                 if p[0] == core:
-                    if p[1] == D:
-                        for t in range(p[2], p[3]):
-                            trs.append((i, gate, T.dd[core * NS + t], T.xd[t]))
-                    else:
-                        trs.append((i, gate, T.rel[:, off:off + p[2] - p[1]], T.xs[:, p[1]:p[2]]))
-                if p[0] != gate and p[1] != D:
+                    trs.append((gate, T.rel[:, off:off + p[2] - p[1]], T.xs[:, p[1]:p[2]], HS[i]))
+                if p[0] != gate:
                     off += p[2] - p[1]
-        dram = any(p[0] == core and p[1] == D for plan in PLAN.values() for p in plan)
-        lq[0].dma_start(T.xd[:] if dram else T.xs[:], T.x[:]).then_inc(s.ld0, 16)
+        g.sync.dma_start(T.xs[:], T.x[:]).then_inc(s.ld0, 16)
         g.wait_ge(s.ld0, 16)
-        fused([(gate, o, i_, HS[i]) for i, gate, o, i_ in trs], 16)
+        fused(trs, 16)
         g.wait_ge(s.sent, 16)
         return
     plan = PLAN[core]
     k = 0
     for i, p in enumerate(plan):
         if p[0] == core:
-            lq[k % 2].dma_start(T.xs[:, p[1]:p[2]], T.x[:, p[1]:p[2]]).then_inc(LD[i], 16)
+            qs[k % 2].dma_start(T.xs[:, p[1]:p[2]], T.x[:, p[1]:p[2]]).then_inc(LD[i], 16)
             k += 1
     off = 0
     for i, p in enumerate(plan):
         blk = p[0]
-        rs = ST[store_of(p)]
+        dst = T.land[:, blk * B + p[1]:blk * B + p[2]]
         if blk == core:
             g.wait_ge(LD[i], 16)
+            src = T.xs[:, p[1]:p[2]]
         else:
-            g.wait_ge(HS[i], hand_engines(blk) * parts(p))
-        if p[1] == D:
-            tr = [(ROOT, T.dd[blk * NS + t], T.dd[blk * NS + t], rs) for t in range(p[2], p[3])]
-        else:
-            dst = T.land[:, blk * B + p[1]:blk * B + p[2]]
-            if blk == core:
-                tr = [(ROOT, dst, T.xs[:, p[1]:p[2]], rs)]
-            else:
-                tr = [(ROOT, dst, T.rel[:, off:off + p[2] - p[1]], rs)]
-                off += p[2] - p[1]
-        fused(tr, width(core))
+            g.wait_ge(HS[i], hand_engines(blk))
+            src = T.rel[:, off:off + p[2] - p[1]]
+            off += p[2] - p[1]
+        fused([(ROOT, dst, src, ST[store_of(p)])], width(core))
     g.wait_ge(s.sent, width(core) * len(plan))

from concourse.bass import DstId, RemoteDMATransfer
B = 512
H = 256
ROOT = 15
PLAN = {
    2: [(2, 0, 256), (2, 256, 512), (0, 0, 256), (4, 0, 256), (5, 0, 256)],
    6: [(6, 0, 256), (6, 256, 512), (0, 256, 512), (4, 256, 512), (5, 256, 512)],
    3: [(3, 0, 256), (3, 256, 512), (1, 0, 256)],
    7: [(7, 0, 256), (7, 256, 512), (1, 256, 512)],
    14: [(14, 0, 256), (14, 256, 512), (12, 0, 512), (10, 0, 512), (8, 0, 256)],
    13: [(13, 256, 512), (13, 0, 256), (11, 0, 512), (9, 0, 512), (8, 256, 512)],
}
STORES = [(13 * B + H, 14 * B + H, 0), (14 * B + H, 15 * B, 0), (13 * B, 13 * B + H, 0),
          (11 * B, 13 * B, 0), (9 * B, 11 * B, 0), (8 * B, 9 * B, 0),
          (6 * B, 8 * B, 1), (2 * B, 4 * B, 1), (0, 2 * B, 1), (4 * B, 5 * B, 1), (5 * B, 6 * B, 1)]
SCRATCH = {'xs': ('sbuf', [128, B], 'bfloat16'), 'rel': ('sbuf', [128, 4 * B], 'bfloat16'),
           'land': ('sbuf', [128, 16 * B], 'bfloat16')}
SEMAPHORES = (['sent', 'stored', 'own'] + ['ld%d' % i for i in range(8)] + ['h%d' % i for i in range(8)]
              + ['st%d' % i for i in range(16)])


def store_of(p):
    for i, st in enumerate(STORES):
        if st[0] <= p[0] * B + p[1] and p[0] * B + p[2] <= st[1]:
            return i
    raise ValueError(p)


def hand_engines(blk):
    return 16 // sum(1 for plan in PLAN.values() for p in plan if p[0] == blk)


def rank_program(g, core, T, topo):
    s = T.sem
    LD = (s.ld0, s.ld1, s.ld2, s.ld3, s.ld4, s.ld5, s.ld6, s.ld7)
    HS = (s.h0, s.h1, s.h2, s.h3, s.h4, s.h5, s.h6, s.h7)
    ST = (s.st0, s.st1, s.st2, s.st3, s.st4, s.st5, s.st6, s.st7, s.st8, s.st9, s.st10, s.st11,
          s.st12, s.st13, s.st14, s.st15)
    qs = (g.sync, g.scalar)

    def width(src):
        return 16 if topo.chip(src) == topo.chip(ROOT) else 8

    def fused(triples, total):
        ne = total // len(triples)
        trs = []
        for k, (dc, out_ap, in_ap, rs) in enumerate(triples):
            rid, pid, _se = topo.addr(dc)
            trs.append(RemoteDMATransfer(dst_ids=[DstId(rid=rid, pnc=pid)],
                                         dma_engine_mask=((1 << ne) - 1) << (ne * k),
                                         remote_sem=rs, src=in_ap, dst=out_ap))
        g.remote_dma_fused(trs, local_sem=s.sent)

    if core == ROOT:
        need = [0] * len(STORES)
        for src, plan in PLAN.items():
            for p in plan:
                need[store_of(p)] += width(src)
        g.dma_start(T.y[:, ROOT * B:(ROOT + 1) * B], T.x[:]).then_inc(s.own, 16)
        for i, st in enumerate(STORES):
            q = qs[st[-1]]
            q.wait_ge(ST[i], need[i])
            q.dma_start(T.y[:, st[0]:st[1]], T.land[:, st[0]:st[1]]).then_inc(s.stored, 16)
        g.wait_ge(s.own, 16)
        g.wait_ge(s.stored, 16 * len(STORES))
        return
    if core not in PLAN:
        trs = []
        for gate, plan in PLAN.items():
            off = 0
            for i, p in enumerate(plan):
                if p[0] == core:
                    trs.append((gate, T.rel[:, off:off + p[2] - p[1]], T.xs[:, p[1]:p[2]], HS[i]))
                if p[0] != gate:
                    off += p[2] - p[1]
        g.sync.dma_start(T.xs[:], T.x[:]).then_inc(s.ld0, 16)
        g.wait_ge(s.ld0, 16)
        fused(trs, 16)
        g.wait_ge(s.sent, 16)
        return
    plan = PLAN[core]
    k = 0
    for i, p in enumerate(plan):
        if p[0] == core:
            qs[k % 2].dma_start(T.xs[:, p[1]:p[2]], T.x[:, p[1]:p[2]]).then_inc(LD[i], 16)
            k += 1
    off = 0
    for i, p in enumerate(plan):
        blk = p[0]
        dst = T.land[:, blk * B + p[1]:blk * B + p[2]]
        if blk == core:
            g.wait_ge(LD[i], 16)
            src = T.xs[:, p[1]:p[2]]
        else:
            g.wait_ge(HS[i], hand_engines(blk))
            src = T.rel[:, off:off + p[2] - p[1]]
            off += p[2] - p[1]
        fused([(ROOT, dst, src, ST[store_of(p)])], width(core))
    g.wait_ge(s.sent, width(core) * len(plan))
